import numpy as np
import ml_dtypes


def mxq(x, axis, fmt="e4m3"):
    dtype, down = {"e4m3": (ml_dtypes.float8_e4m3fn, 7), "e5m2": (ml_dtypes.float8_e5m2, 14)}[fmt]
    v = np.moveaxis(np.asarray(x, np.float32).astype(ml_dtypes.bfloat16).astype(np.float64), axis, -1)
    blocks = v.reshape(v.shape[:-1] + (-1, 32))
    amax = np.abs(blocks).max(-1, keepdims=True)
    byte = np.maximum(np.where(amax > 0, np.frexp(amax)[1] - 1 + 127, 0) - down, 1)
    scale = np.exp2(byte - 127.0)
    codes = (blocks / scale).astype(np.float32).astype(dtype).astype(np.float64)
    return np.moveaxis((codes * scale).reshape(v.shape), -1, axis)


WIDE = False


def mx_kscale(k):
    if not WIDE:
        return np.ones(k)
    levels = np.array([10, -10, 5, -5, 0])
    if k % 512:
        return np.exp2(np.random.permutation(np.resize(levels, k // 32))).repeat(32)
    a = np.empty((k // 512, 16))
    for p in range(k // 512):
        a[p, :8] = np.random.permutation(np.resize(levels, 8))
        for g in range(8):
            far = levels[np.abs(levels - a[p, g]) >= 10]
            a[p, g + 8] = far[np.random.randint(len(far))]
    return np.exp2(a.ravel()).repeat(32)


def f64(x):
    return np.asarray(x).astype(np.float64)


def striped(idx):
    return np.tile(idx.reshape(-1, 16).T, (8, 1)).astype(np.uint16)


def unstriped(offs):
    return offs[:16].T.reshape(-1).astype(np.int64)


E2M1 = np.array([0.0, 0.5, 1.0, 1.5, 2.0, 3.0, 4.0, 6.0, -0.0, -0.5, -1.0, -1.5, -2.0, -3.0, -4.0, -6.0])


def pack_weight(w, fmt):
    k, n = w.shape
    w = f64(np.asarray(w, np.float32).astype(ml_dtypes.bfloat16)).reshape(k // 32, 32, n)
    amax = np.abs(w).max(1)
    if fmt == "e4m3":
        byte = np.frexp(amax)[1] - 1 + 127 - 7
    else:
        mant, ex = np.frexp(amax / 6.0)
        byte = np.where(mant > 0.5, ex, ex - 1) + 127
    byte = np.clip(np.where(amax > 0, byte, 1), 1, 254)
    scaled = (w * np.exp2(127.0 - byte)[:, None, :]).reshape(k, n).astype(np.float32)
    by_word = np.ascontiguousarray(scaled.reshape(k // 512, 128, 4, n).transpose(0, 1, 3, 2))
    if fmt == "e4m3":
        words = by_word.astype(ml_dtypes.float8_e4m3fn).view(np.uint8)
    else:
        c = by_word.astype(ml_dtypes.float4_e2m1fn).view(np.uint8) & 0xF
        words = (c[..., 0::2] | (c[..., 1::2] << 4)).reshape(k // 512, 128, 2 * n)
    return np.ascontiguousarray(words), np.ascontiguousarray(byte.astype(np.uint8).reshape(k // 512, 16, n))


def unpack_weight(words, scales, fmt):
    g, _, n = scales.shape
    words = np.ascontiguousarray(words).reshape(g, 128, n, -1)
    if fmt == "e4m3":
        vals = words.view(ml_dtypes.float8_e4m3fn).astype(np.float64)
    else:
        nib = np.empty((g, 128, n, 4), np.uint8)
        nib[..., 0::2] = words & 0xF
        nib[..., 1::2] = words >> 4
        vals = E2M1[nib]
    vals = vals * np.repeat(np.exp2(scales.astype(np.float64) - 127.0), 8, axis=1)[..., None]
    return vals.transpose(0, 1, 3, 2).reshape(g * 512, n)


def gelu(v):
    return 0.5 * v * (1.0 + np.tanh(np.sqrt(2.0 / np.pi) * (v + 0.044715 * v**3)))


K, H, N, T, S, T2, P = 512, 1024, 512, 4096, 1024, 2048, 1024


def setup_inputs():
    n = np.random.standard_normal
    s = mx_kscale(K)[:, None]
    u = mx_kscale(H)[:, None]
    d = {}
    d["tab_words"], d["tab_scales"] = pack_weight(n((K, T)) * s, "e4m3")
    d["offs"] = striped(np.random.permutation(T)[:S])
    d["offs2"] = striped(np.random.permutation(T2)[:S])
    d["offs3"] = striped(np.random.permutation(T2)[:P])
    d["offs4"] = striped(np.random.permutation(T2)[:P])
    d["w1"] = (n((K, H)) / K**0.5 / s).astype(np.float32)
    d["w2"] = (n((K, H)) / K**0.5 / s).astype(np.float32)
    d["w3_words"], d["w3_scales"] = pack_weight(n((K, H)) / K**0.5 / s, "e2m1")
    d["gain"] = (np.exp(0.3 * n(H)) * u[:, 0]).astype(np.float32)
    d["wgs"] = np.exp(0.3 * n((128, S))).astype(np.float32)
    d["page0"] = (n((H, T2)) * u).astype(np.float32)
    d["rest"] = (0.6 * n(H) * u[:, 0]).astype(np.float32)
    d["w4_words"], d["w4_scales"] = pack_weight(1.3 * n((H, N)) / H**0.5 / u, "e4m3")
    d["wgo"] = np.exp(0.3 * n((128, P))).astype(np.float32)
    d["page1"] = (1.5 * n((N, T2))).astype(np.float32)
    return d


def reference(tab_words, tab_scales, offs, offs2, offs3, offs4, w1, w2, w3_words, w3_scales,
              gain, wgs, page0, rest, w4_words, w4_scales, wgo, page1):
    v = unpack_weight(tab_words, tab_scales, "e4m3")[:, unstriped(offs)]
    a = mxq(f64(w1), 0, "e4m3").T @ v
    b = mxq(f64(w2), 0, "e4m3").T @ v
    e = unpack_weight(w3_words, w3_scales, "e2m1").T @ v
    h = f64(gain)[:, None] * np.maximum(np.maximum(a, b), e)
    page = f64(page0).copy()
    page[:, unstriped(offs2)] = np.tile(f64(wgs), (H // 128, 1)) * h
    x = page[:, unstriped(offs3)] - f64(rest)[:, None]
    y = np.sqrt(np.square(unpack_weight(w4_words, w4_scales, "e4m3").T @ mxq(x, 0, "e4m3")) + 1.0)
    out = f64(page1).copy()
    out[:, unstriped(offs4)] = np.tile(f64(wgo), (N // 128, 1)) * y
    return out

@@ -1,0 +1,246 @@
+from contextlib import ExitStack
+
+import concourse.mybir as mybir
+
+K, H, N, T, S, T2, PK = 512, 1024, 512, 4096, 1024, 2048, 1024
+FLOPS = 2 * (3 * K * H * S + H * N * PK)
+
+F32 = mybir.dt.float32
+BF16 = mybir.dt.bfloat16
+I32 = mybir.dt.int32
+U32 = mybir.dt.uint32
+U16 = mybir.dt.uint16
+U8 = mybir.dt.uint8
+FP8X4 = mybir.dt.float8_e4m3fn_x4
+FP4X4 = mybir.dt.float4_e2m1fn_x4
+ACT = mybir.ActivationFunctionType
+ALU = mybir.AluOpType
+
+P = 128
+HALF = 512
+LIST_HALF = HALF // 16
+
+
+def tile_list_crane_sway_page_kernel(tc, tab_words, tab_scales, offs, offs2, offs3, offs4, w1, w2,
+                                              w3_words, w3_scales, gain, wgs, page0, rest, w4_words,
+                                              w4_scales, wgo, page1, out):
+    nc = tc.nc
+    with ExitStack() as ctx:
+        lists = ctx.enter_context(tc.tile_pool(name="lists", bufs=1))
+        sb = ctx.enter_context(tc.tile_pool(name="sb", bufs=1))
+        ps = ctx.enter_context(tc.psum_pool(name="ps", bufs=2))
+
+        def tile(name, shape, dtype, tag=None, bufs=1):
+            return sb.tile(shape, dtype, name=name, tag=tag or name, bufs=bufs, align_bytes=64)
+
+        def half(h):
+            return slice(h * HALF, (h + 1) * HALF)
+
+        def list_half(lst, h):
+            return lst[:, h * LIST_HALF:(h + 1) * LIST_HALF]
+
+        def load_scale_rows(queue, plane, rows):
+            for q in range(4):
+                queue.dma_start(out=plane[32 * q:32 * q + 4].bitcast(I32), in_=rows[4 * q:4 * q + 4].bitcast(I32))
+
+        idx1 = lists.tile([P, S // 16], U16, name="idx1")
+        idx2 = lists.tile([P, S // 16], U16, name="idx2")
+        idx3 = lists.tile([P, PK // 16], U16, name="idx3")
+        idx4 = lists.tile([P, PK // 16], U16, name="idx4")
+
+        tab_s = tile("tab_s", [P, T], U8)
+        w3_s_raw = tile("w3_s_raw", [P, H], U8)
+        w4_s = tile("w4_s", [P, 2, N], U8)
+        one = tile("one", [P, 1], F32)
+        one_b = tile("one_b", [P, 1], F32)
+        nc.vector.memset(tab_s[:].bitcast(I32), 0)
+        nc.vector.memset(one[:], 1.0)
+        nc.vector.memset(w3_s_raw[:].bitcast(I32), 0)
+        nc.vector.memset(w4_s[:].rearrange("p a n -> p (a n)").bitcast(I32), 0)
+        nc.scalar.activation(one_b[:], one[:], ACT.Sqrt)
+
+        nc.sync.dma_start(idx1[:], offs)
+        load_scale_rows(nc.gpsimd, tab_s, tab_scales[0])
+        load_scale_rows(nc.gpsimd, w3_s_raw, w3_scales[0])
+        w3_w_raw = tile("w3_w_raw", [P, 2 * H], U8)
+        nc.sync.dma_start(out=w3_w_raw[:].bitcast(I32), in_=w3_words[0].bitcast(I32))
+
+        def load_w(w, which, b):
+            raw = tile("w_raw%d_%d" % (which, b), [P, 4, HALF], F32, tag="w_raw%d" % which)
+            nc.sync.dma_start(out=raw[:], in_=w[:, half(b)].rearrange("(p j) c -> p j c", j=4))
+            return raw
+
+        def cast_w(raw, which, b):
+            grouped = tile("w_bf%d_%d" % (which, b), [P, 4 * HALF], BF16, tag="w_bf%d" % which)
+            nc.scalar.copy(out=grouped[:].rearrange("p (t m j) -> p m t j", t=4, j=4),
+                           in_=raw[:].rearrange("p j (m t) -> p m t j", t=4))
+            return grouped
+
+        w_raw = [load_w(w1, 0, 0), load_w(w2, 1, 0)]
+        tab_w = tile("tab_w", [P, T], U32)
+        nc.sync.dma_start(out=tab_w[:].bitcast(I32), in_=tab_words[0].rearrange("p t i -> p (t i)").bitcast(I32))
+
+
+        gain_t = tile("gain_t", [P, 2, 4], F32)
+        nc.sync.dma_start(out=gain_t[:], in_=gain.rearrange("(b p t) -> p b t", b=2, t=4))
+        wgs_rows = wgs.rearrange("(q t) j -> q t j", t=4)
+        wgs_first = tile("wgs_first", [P, S], F32)
+        for q in range(4):
+            nc.sync.dma_start(out=wgs_first[32 * q:32 * q + 32, :], in_=wgs_rows[:, 0, :])
+        page0_rows = page0.rearrange("(b p t) c -> b t p c", b=2, t=4)
+        pages = [tile("page%d" % r, [P, T2], F32) for r in range(8)]
+        nc.sync.dma_start(out=pages[0][:], in_=page0_rows[0, 0])
+        nc.sync.dma_start(idx2[:], offs2)
+
+        v_s = [tile("v_s%d" % h, [P, HALF], U8) for h in range(2)]
+        v_w = [tile("v_w%d" % h, [P, HALF], U32) for h in range(2)]
+        for h in range(2):
+            nc.vector.tensor_copy(v_s[h][:], tab_s[:].indirect(list_half(idx1, h)))
+        w3_w = tile("w3_w", [P, 2 * H], U8)
+        w3_s = tile("w3_s", [P, H], U8)
+        nc.vector.tensor_copy(w3_w[:].rearrange("p (b t q e) -> p b q t e", b=2, t=4, e=2),
+                              w3_w_raw[:].rearrange("p (b q t e) -> p b q t e", b=2, t=4, e=2))
+        nc.vector.tensor_copy(w3_s[:].rearrange("p (b t q) -> p b t q", b=2, t=4),
+                              w3_s_raw[:].rearrange("p (b q t) -> p b t q", b=2, t=4))
+
+        w_s = tile("w_s", [P, 2, 2, HALF], U8)
+        w_c = {}
+
+        def quantize_w(grouped, b, tag):
+            w_c[b] = tile("w_c%d" % b, [P, 2, HALF], U32, tag=tag)
+            for which in range(2):
+                nc.vector.quantize_mx(out=w_c[b][:, which, :].bitcast(FP8X4), scales=w_s[:, b, which, :],
+                                      in_=grouped[which][:])
+
+        quantize_w([cast_w(w_raw[0], 0, 0), cast_w(w_raw[1], 1, 0)], 0, "w_c0")
+        for h in range(2):
+            nc.vector.tensor_copy(v_w[h][:], tab_w[:].indirect(list_half(idx1, h)))
+
+        wgs_other = tile("wgs_other", [P, 3, S], F32)
+        for q in range(4):
+            nc.sync.dma_start(out=wgs_other[32 * q:32 * q + 32], in_=wgs_rows[:, 1:4, :])
+        nc.sync.dma_start(idx3[:], offs3)
+        rest_t = tile("rest_t", [P, 2, 4], F32)
+        nc.sync.dma_start(out=rest_t[:], in_=rest.rearrange("(b p t) -> p b t", b=2, t=4))
+        nc.sync.dma_start(out=pages[1][:], in_=page0_rows[0, 1])
+        w_raw = [load_w(w1, 0, 1), load_w(w2, 1, 1)]
+        for r in range(2, 8):
+            nc.sync.dma_start(out=pages[r][:], in_=page0_rows[r // 4, r % 4])
+        nc.sync.dma_start(idx4[:], offs4)
+        load_scale_rows(nc.sync, w4_s, w4_scales.rearrange("a q n -> q a n"))
+        w4_w = tile("w4_w", [P, 2, N], U32)
+        nc.sync.dma_start(out=w4_w[:].bitcast(I32), in_=w4_words.rearrange("a p c i -> p a (c i)").bitcast(I32))
+        wgo_t = tile("wgo_t", [P, PK], F32)
+        nc.sync.dma_start(out=wgo_t[:], in_=wgo)
+        outs = [tile("out%d" % n, [P, T2], F32) for n in range(4)]
+        for n in range(4):
+            nc.sync.dma_start(out=outs[n][:], in_=page1[n * P:(n + 1) * P, :])
+
+        neg_rest = tile("neg_rest", [P, 8], F32)
+
+        def largest(r):
+            b, t = divmod(r, 4)
+            cols = slice(t * P, (t + 1) * P)
+            top = tile("top%d" % r, [P, S], F32, tag="top")
+            banks = []
+            for h in range(2):
+                pa = ps.tile([P, HALF], F32, name="pa%d_%d" % (r, h), tag="pa")
+                pb = ps.tile([P, HALF], F32, name="pb%d_%d" % (r, h), tag="pb")
+                pe = ps.tile([P, HALF], F32, name="pe%d_%d" % (r, h), tag="pe")
+                for which, bank in ((0, pa), (1, pb)):
+                    nc.tensor.matmul_mx(out=bank[:], lhsT=w_c[b][:, which, cols].bitcast(FP8X4),
+                                        lhsT_scale=w_s[:, b, which, cols], rhs=v_w[h][:].bitcast(FP8X4),
+                                        rhs_scale=v_s[h][:], start=True, stop=True)
+                nc.tensor.matmul_mx(out=pe[:], lhsT=w3_w[:, 2 * r * P:2 * (r + 1) * P].bitcast(FP4X4),
+                                    lhsT_scale=w3_s[:, r * P:(r + 1) * P], rhs=v_w[h][:].bitcast(FP8X4),
+                                    rhs_scale=v_s[h][:], start=True, stop=True)
+                a_sb = tile("a_sb%d_%d" % (r, h), [P, HALF], F32, tag="a_sb", bufs=2)
+                nc.scalar.copy(out=a_sb[:], in_=pa[:])
+                banks.append((a_sb, pb, pe))
+            for h in range(2):
+                nc.vector.tensor_tensor(top[:, half(h)], banks[h][0][:], banks[h][1][:], ALU.max)
+            for h in range(2):
+                nc.vector.tensor_tensor(top[:, half(h)], top[:, half(h)], banks[h][2][:], ALU.max)
+            return top
+
+        def weight(r):
+            b, t = divmod(r, 4)
+            wg = tile("wg%d" % r, [P, S], F32, tag="slot%d" % r)
+            src = wgs_first[:] if t == 0 else wgs_other[:, t - 1, :]
+            nc.scalar.activation(wg[:], src, ACT.Copy, scale=gain_t[:, b, t:t + 1])
+            return wg
+
+        def against_rest(x_bf, picked, r):
+            nc.scalar.activation(x_bf.rearrange("p (j t) -> p j t", t=4)[:, :, r % 4], picked, ACT.Identity,
+                                 bias=neg_rest[:, r:r + 1])
+
+        top = largest(0)
+        x_bf = {}
+        for r in range(8):
+            wg = weight(r)
+            nc.vector.tensor_tensor(pages[r][:].indirect(idx2[:]), top[:], wg[:], ALU.mult)
+            if r == 0:
+                nc.scalar.activation(neg_rest[:], rest_t[:].rearrange("p b t -> p (b t)"), ACT.Copy, scale=-1.0)
+                w_bf = [cast_w(w_raw[0], 0, 1), cast_w(w_raw[1], 1, 1)]
+                x_bf[0] = tile("x_bf0", [P, 4 * PK], BF16, tag="w_raw0")
+            if r < 7:
+                if r == 3:
+                    x_bf[1, 0] = tile("x_bf1_0", [P, 4 * HALF], BF16, tag="w_bf0")
+                top = largest(r + 1)
+            if r == 2:
+                quantize_w(w_bf, 1, "slot2")
+            picked = tile("picked%d" % r, [P, PK], F32, tag="picked", bufs=2)
+            if r < 4:
+                nc.vector.tensor_copy(picked[:], pages[r][:].indirect(idx3[:]))
+                against_rest(x_bf[0][:], picked[:], r)
+            else:
+                nc.vector.tensor_copy(picked[:, half(0)], pages[r][:].indirect(list_half(idx3, 0)))
+                against_rest(x_bf[1, 0][:], picked[:, half(0)], r)
+
+        x_c = [tile("x_c0", [P, PK], U32, tag="slot7"), tile("x_c1", [P, PK], U32, tag="slot5")]
+        x_s = tile("x_s", [P, 2, PK], U8)
+
+        def quantize_x(a, h, grouped):
+            nc.vector.quantize_mx(out=x_c[a][:, half(h)].bitcast(FP8X4), scales=x_s[:, a, half(h)], in_=grouped)
+
+        def late_gathers(rows, tag):
+            late = tile("late%d" % rows[0], [P, 2, HALF], F32, tag=tag)
+            for i, r in enumerate(rows):
+                nc.vector.tensor_copy(late[:, i, :], pages[r][:].indirect(list_half(idx3, 1)))
+            return late
+
+        quantize_x(0, 0, x_bf[0][:, 0:4 * HALF])
+        late45 = late_gathers((4, 5), "top")
+        quantize_x(1, 0, x_bf[1, 0][:])
+        quantize_x(0, 1, x_bf[0][:, 4 * HALF:8 * HALF])
+        late67 = late_gathers((6, 7), "w_bf0")
+
+        def squares(n, h, tag, bufs):
+            z = ps.tile([P, HALF], F32, name="z%d_%d" % (n, h), tag="z")
+            cols = slice(n * P, (n + 1) * P)
+            for a in range(2):
+                nc.tensor.matmul_mx(out=z[:], lhsT=w4_w[:, a, cols].bitcast(FP8X4), lhsT_scale=w4_s[:, a, cols],
+                                    rhs=x_c[a][:, half(h)].bitcast(FP8X4), rhs_scale=x_s[:, a, half(h)],
+                                    start=(a == 0), stop=(a == 1))
+            sq = tile("sq%d_%d" % (n, h), [P, HALF], F32, tag=tag, bufs=bufs)
+            nc.scalar.activation(sq[:], z[:], ACT.Square)
+            return sq
+
+        def place(n, h, sq, tag):
+            y = tile("y%d_%d" % (n, h), [P, HALF], F32, tag=tag)
+            nc.scalar.activation(y[:], sq[:], ACT.Sqrt, bias=one_b[:])
+            nc.vector.tensor_tensor(outs[n][:].indirect(list_half(idx4, h)), y[:], wgo_t[:, half(h)], ALU.mult)
+
+        y_tags = ("slot0", "slot1", "slot3", "slot4")
+        place(0, 0, squares(0, 0, "slot6", 1), y_tags[0])
+        for n in (1, 2):
+            place(n, 0, squares(n, 0, "a_sb", 2), y_tags[n])
+        sq_last = squares(3, 0, "a_sb", 2)
+        x_bf[1, 1] = tile("x_bf1_1", [P, 4 * HALF], BF16, tag="slot6")
+        for r in range(4, 8):
+            against_rest(x_bf[1, 1][:], (late45 if r < 6 else late67)[:, r % 2, :], r)
+        quantize_x(1, 1, x_bf[1, 1][:])
+        place(3, 0, sq_last, "slot6")
+        for n in range(4):
+            place(n, 1, squares(n, 1, "a_sb", 2), y_tags[n])
+            nc.sync.dma_start(out=out[n * P:(n + 1) * P, :], in_=outs[n][:])

@@ -19,6 +19,7 @@ ALU = mybir.AluOpType
 P = 128
 HALF = 512
 LIST_HALF = HALF // 16
+WG_SLOT = (None, "w_bf1", "slot_x", "slot_y", "slot_z", "slot_y", "slot_z", "slot_y")
 
 
 def tile_list_crane_sway_page_kernel(tc, tab_words, tab_scales, offs, offs2, offs3, offs4, w1, w2,
@@ -53,17 +54,12 @@ def tile_list_crane_sway_page_kernel(tc, tab_words, tab_scales, offs, offs2, off
         w4_s = tile("w4_s", [P, 2, N], U8)
         one = tile("one", [P, 1], F32)
         one_b = tile("one_b", [P, 1], F32)
-        nc.vector.memset(tab_s[:].bitcast(I32), 0)
-        nc.vector.memset(one[:], 1.0)
+        nc.gpsimd.memset(tab_s[:, 0:T // 2].bitcast(I32), 0)
+        nc.vector.memset(tab_s[:, T // 2:T].bitcast(I32), 0)
         nc.vector.memset(w3_s_raw[:].bitcast(I32), 0)
-        nc.vector.memset(w4_s[:].rearrange("p a n -> p (a n)").bitcast(I32), 0)
+        nc.gpsimd.memset(one[:], 1.0)
+        nc.gpsimd.memset(w4_s[:].rearrange("p a n -> p (a n)").bitcast(I32), 0)
         nc.scalar.activation(one_b[:], one[:], ACT.Sqrt)
-
-        nc.sync.dma_start(idx1[:], offs)
-        load_scale_rows(nc.gpsimd, tab_s, tab_scales[0])
-        load_scale_rows(nc.gpsimd, w3_s_raw, w3_scales[0])
-        w3_w_raw = tile("w3_w_raw", [P, 2 * H], U8)
-        nc.sync.dma_start(out=w3_w_raw[:].bitcast(I32), in_=w3_words[0].bitcast(I32))
 
         def load_w(w, which, b):
             raw = tile("w_raw%d_%d" % (which, b), [P, 4, HALF], F32, tag="w_raw%d" % which)
@@ -76,30 +72,34 @@ def tile_list_crane_sway_page_kernel(tc, tab_words, tab_scales, offs, offs2, off
                            in_=raw[:].rearrange("p j (m t) -> p m t j", t=4))
             return grouped
 
-        w_raw = [load_w(w1, 0, 0), load_w(w2, 1, 0)]
-        tab_w = tile("tab_w", [P, T], U32)
-        nc.sync.dma_start(out=tab_w[:].bitcast(I32), in_=tab_words[0].rearrange("p t i -> p (t i)").bitcast(I32))
-
-
         gain_t = tile("gain_t", [P, 2, 4], F32)
-        nc.sync.dma_start(out=gain_t[:], in_=gain.rearrange("(b p t) -> p b t", b=2, t=4))
+        rest_t = tile("rest_t", [P, 2, 4], F32)
+        w3_w_raw = tile("w3_w_raw", [P, 2 * H], U8)
+        tab_w = tile("tab_w", [P, T], U32)
         wgs_rows = wgs.rearrange("(q t) j -> q t j", t=4)
         wgs_first = tile("wgs_first", [P, S], F32)
-        for q in range(4):
-            nc.sync.dma_start(out=wgs_first[32 * q:32 * q + 32, :], in_=wgs_rows[:, 0, :])
         page0_rows = page0.rearrange("(b p t) c -> b t p c", b=2, t=4)
         pages = [tile("page%d" % r, [P, T2], F32) for r in range(8)]
+        nc.sync.dma_start(idx1[:], offs)
+        nc.sync.dma_start(out=w3_w_raw[:].bitcast(I32), in_=w3_words[0].bitcast(I32))
+        load_scale_rows(nc.sync, tab_s, tab_scales[0])
+        w_raw = [load_w(w1, 0, 0), load_w(w2, 1, 0)]
+        load_scale_rows(nc.sync, w3_s_raw, w3_scales[0])
+        nc.sync.dma_start(out=tab_w[:].bitcast(I32), in_=tab_words[0].rearrange("p t i -> p (t i)").bitcast(I32))
+        nc.sync.dma_start(out=gain_t[:], in_=gain.rearrange("(b p t) -> p b t", b=2, t=4))
+        for q in range(4):
+            nc.sync.dma_start(out=wgs_first[32 * q:32 * q + 32, :], in_=wgs_rows[:, 0, :])
         nc.sync.dma_start(out=pages[0][:], in_=page0_rows[0, 0])
         nc.sync.dma_start(idx2[:], offs2)
 
         v_s = [tile("v_s%d" % h, [P, HALF], U8) for h in range(2)]
         v_w = [tile("v_w%d" % h, [P, HALF], U32) for h in range(2)]
-        for h in range(2):
-            nc.vector.tensor_copy(v_s[h][:], tab_s[:].indirect(list_half(idx1, h)))
         w3_w = tile("w3_w", [P, 2 * H], U8)
         w3_s = tile("w3_s", [P, H], U8)
         nc.vector.tensor_copy(w3_w[:].rearrange("p (b t q e) -> p b q t e", b=2, t=4, e=2),
                               w3_w_raw[:].rearrange("p (b q t e) -> p b q t e", b=2, t=4, e=2))
+        for h in range(2):
+            nc.vector.tensor_copy(v_s[h][:], tab_s[:].indirect(list_half(idx1, h)))
         nc.vector.tensor_copy(w3_s[:].rearrange("p (b t q) -> p b t q", b=2, t=4),
                               w3_s_raw[:].rearrange("p (b q t) -> p b t q", b=2, t=4))
 
@@ -119,14 +119,13 @@ def tile_list_crane_sway_page_kernel(tc, tab_words, tab_scales, offs, offs2, off
         wgs_other = tile("wgs_other", [P, 3, S], F32)
         for q in range(4):
             nc.sync.dma_start(out=wgs_other[32 * q:32 * q + 32], in_=wgs_rows[:, 1:4, :])
-        nc.sync.dma_start(idx3[:], offs3)
-        rest_t = tile("rest_t", [P, 2, 4], F32)
-        nc.sync.dma_start(out=rest_t[:], in_=rest.rearrange("(b p t) -> p b t", b=2, t=4))
         nc.sync.dma_start(out=pages[1][:], in_=page0_rows[0, 1])
+        nc.sync.dma_start(idx3[:], offs3)
+        nc.sync.dma_start(out=rest_t[:], in_=rest.rearrange("(b p t) -> p b t", b=2, t=4))
+        nc.sync.dma_start(idx4[:], offs4)
         w_raw = [load_w(w1, 0, 1), load_w(w2, 1, 1)]
         for r in range(2, 8):
             nc.sync.dma_start(out=pages[r][:], in_=page0_rows[r // 4, r % 4])
-        nc.sync.dma_start(idx4[:], offs4)
         load_scale_rows(nc.sync, w4_s, w4_scales.rearrange("a q n -> q a n"))
         w4_w = tile("w4_w", [P, 2, N], U32)
         nc.sync.dma_start(out=w4_w[:].bitcast(I32), in_=w4_words.rearrange("a p c i -> p a (c i)").bitcast(I32))
@@ -141,7 +140,6 @@ def tile_list_crane_sway_page_kernel(tc, tab_words, tab_scales, offs, offs2, off
         def largest(r):
             b, t = divmod(r, 4)
             cols = slice(t * P, (t + 1) * P)
-            top = tile("top%d" % r, [P, S], F32, tag="top")
             banks = []
             for h in range(2):
                 pa = ps.tile([P, HALF], F32, name="pa%d_%d" % (r, h), tag="pa")
@@ -154,42 +152,61 @@ def tile_list_crane_sway_page_kernel(tc, tab_words, tab_scales, offs, offs2, off
                 nc.tensor.matmul_mx(out=pe[:], lhsT=w3_w[:, 2 * r * P:2 * (r + 1) * P].bitcast(FP4X4),
                                     lhsT_scale=w3_s[:, r * P:(r + 1) * P], rhs=v_w[h][:].bitcast(FP8X4),
                                     rhs_scale=v_s[h][:], start=True, stop=True)
-                a_sb = tile("a_sb%d_%d" % (r, h), [P, HALF], F32, tag="a_sb", bufs=2)
-                nc.scalar.copy(out=a_sb[:], in_=pa[:])
+                if r == 0:
+                    a_sb = a_first[:, half(h)]
+                else:
+                    a_sb = tile("a_sb%d_%d" % (r, h), [P, HALF], F32, tag="a_sb", bufs=2)[:]
+                nc.scalar.copy(out=a_sb, in_=pa[:])
                 banks.append((a_sb, pb, pe))
-            for h in range(2):
-                nc.vector.tensor_tensor(top[:, half(h)], banks[h][0][:], banks[h][1][:], ALU.max)
-            for h in range(2):
-                nc.vector.tensor_tensor(top[:, half(h)], top[:, half(h)], banks[h][2][:], ALU.max)
-            return top
+            return banks
 
-        def weight(r):
+        def maxima(tops, banks):
+            for top, (a_sb, pb, pe) in zip(tops, banks):
+                nc.vector.tensor_tensor(top, a_sb, pb[:], ALU.max)
+            for top, (a_sb, pb, pe) in zip(tops, banks):
+                nc.vector.tensor_tensor(top, top, pe[:], ALU.max)
+
+        def weight(wg, r):
             b, t = divmod(r, 4)
-            wg = tile("wg%d" % r, [P, S], F32, tag="slot%d" % r)
             src = wgs_first[:] if t == 0 else wgs_other[:, t - 1, :]
-            nc.scalar.activation(wg[:], src, ACT.Copy, scale=gain_t[:, b, t:t + 1])
-            return wg
+            nc.scalar.activation(wg, src, ACT.Copy, scale=gain_t[:, b, t:t + 1])
 
         def against_rest(x_bf, picked, r):
             nc.scalar.activation(x_bf.rearrange("p (j t) -> p j t", t=4)[:, :, r % 4], picked, ACT.Identity,
                                  bias=neg_rest[:, r:r + 1])
 
-        top = largest(0)
+        a_first = tile("a_first", [P, S], F32, tag="w_bf1")
+        banks = largest(0)
+        for h in range(2):
+            top = tile("top0_%d" % h, [P, HALF], F32, tag=("top1", "slot_x")[h])
+            wg = tile("wg0_%d" % h, [P, HALF], F32, tag=("slot_x", "w_bf0")[h])
+            nc.gpsimd.tensor_scalar(wg[:], wgs_first[:, half(h)], gain_t[:, 0, 0:1], 0.0, ALU.mult, ALU.add)
+            maxima([top[:]], banks[h:h + 1])
+            nc.vector.tensor_tensor(pages[0][:].indirect(list_half(idx2, h)), top[:], wg[:], ALU.mult)
         x_bf = {}
         for r in range(8):
-            wg = weight(r)
-            nc.vector.tensor_tensor(pages[r][:].indirect(idx2[:]), top[:], wg[:], ALU.mult)
+            if r > 0:
+                wg = tile("wg%d" % r, [P, S], F32, tag=WG_SLOT[r])
+                weight(wg[:], r)
+                nc.vector.tensor_tensor(pages[r][:].indirect(idx2[:]), top[:], wg[:], ALU.mult)
             if r == 0:
-                nc.scalar.activation(neg_rest[:], rest_t[:].rearrange("p b t -> p (b t)"), ACT.Copy, scale=-1.0)
-                w_bf = [cast_w(w_raw[0], 0, 1), cast_w(w_raw[1], 1, 1)]
+                nc.gpsimd.tensor_scalar(neg_rest[:], rest_t[:].rearrange("p b t -> p (b t)"), -1.0, 0.0, ALU.mult, ALU.add)
+                w_bf = [cast_w(w_raw[0], 0, 1)]
                 x_bf[0] = tile("x_bf0", [P, 4 * PK], BF16, tag="w_raw0")
+            if r == 1:
+                w_bf.append(cast_w(w_raw[1], 1, 1))
             if r < 7:
                 if r == 3:
                     x_bf[1, 0] = tile("x_bf1_0", [P, 4 * HALF], BF16, tag="w_bf0")
-                top = largest(r + 1)
+                banks = largest(r + 1)
+                top = tile("top%d" % (r + 1), [P, S], F32, tag="top%d" % ((r + 1) % 2))
+                maxima([top[:, half(0)], top[:, half(1)]], banks)
             if r == 2:
-                quantize_w(w_bf, 1, "slot2")
-            picked = tile("picked%d" % r, [P, PK], F32, tag="picked", bufs=2)
+                quantize_w(w_bf, 1, "slot_x")
+            if r < 2:
+                picked = tile("picked%d" % r, [P, PK], F32, tag=("slot_y", "slot_z")[r])
+            else:
+                picked = tile("picked%d" % r, [P, PK], F32, tag="picked", bufs=2)
             if r < 4:
                 nc.vector.tensor_copy(picked[:], pages[r][:].indirect(idx3[:]))
                 against_rest(x_bf[0][:], picked[:], r)
@@ -197,7 +214,7 @@ def tile_list_crane_sway_page_kernel(tc, tab_words, tab_scales, offs, offs2, off
                 nc.vector.tensor_copy(picked[:, half(0)], pages[r][:].indirect(list_half(idx3, 0)))
                 against_rest(x_bf[1, 0][:], picked[:, half(0)], r)
 
-        x_c = [tile("x_c0", [P, PK], U32, tag="slot7"), tile("x_c1", [P, PK], U32, tag="slot5")]
+        x_c = [tile("x_c0", [P, PK], U32, tag="slot_y"), tile("x_c1", [P, PK], U32)]
         x_s = tile("x_s", [P, 2, PK], U8)
 
         def quantize_x(a, h, grouped):
@@ -210,7 +227,7 @@ def tile_list_crane_sway_page_kernel(tc, tab_words, tab_scales, offs, offs2, off
             return late
 
         quantize_x(0, 0, x_bf[0][:, 0:4 * HALF])
-        late45 = late_gathers((4, 5), "top")
+        late45 = late_gathers((4, 5), "top1")
         quantize_x(1, 0, x_bf[1, 0][:])
         quantize_x(0, 1, x_bf[0][:, 4 * HALF:8 * HALF])
         late67 = late_gathers((6, 7), "w_bf0")
@@ -231,16 +248,16 @@ def tile_list_crane_sway_page_kernel(tc, tab_words, tab_scales, offs, offs2, off
             nc.scalar.activation(y[:], sq[:], ACT.Sqrt, bias=one_b[:])
             nc.vector.tensor_tensor(outs[n][:].indirect(list_half(idx4, h)), y[:], wgo_t[:, half(h)], ALU.mult)
 
-        y_tags = ("slot0", "slot1", "slot3", "slot4")
-        place(0, 0, squares(0, 0, "slot6", 1), y_tags[0])
+        y_tags = ("y0", "y1", "y2", "y3")
+        place(0, 0, squares(0, 0, "slot_z", 1), y_tags[0])
         for n in (1, 2):
             place(n, 0, squares(n, 0, "a_sb", 2), y_tags[n])
         sq_last = squares(3, 0, "a_sb", 2)
-        x_bf[1, 1] = tile("x_bf1_1", [P, 4 * HALF], BF16, tag="slot6")
+        x_bf[1, 1] = tile("x_bf1_1", [P, 4 * HALF], BF16, tag="slot_z")
         for r in range(4, 8):
             against_rest(x_bf[1, 1][:], (late45 if r < 6 else late67)[:, r % 2, :], r)
         quantize_x(1, 1, x_bf[1, 1][:])
-        place(3, 0, sq_last, "slot6")
+        place(3, 0, sq_last, "slot_z")
         for n in range(4):
             place(n, 1, squares(n, 1, "a_sb", 2), y_tags[n])
             nc.sync.dma_start(out=out[n * P:(n + 1) * P, :], in_=outs[n][:])

from contextlib import ExitStack

import concourse.mybir as mybir

K, H, N, T, S, T2, PK = 512, 1024, 512, 4096, 1024, 2048, 1024
FLOPS = 2 * (3 * K * H * S + H * N * PK)

F32 = mybir.dt.float32
BF16 = mybir.dt.bfloat16
I32 = mybir.dt.int32
U32 = mybir.dt.uint32
U16 = mybir.dt.uint16
U8 = mybir.dt.uint8
FP8X4 = mybir.dt.float8_e4m3fn_x4
FP4X4 = mybir.dt.float4_e2m1fn_x4
ACT = mybir.ActivationFunctionType
ALU = mybir.AluOpType

P = 128
HALF = 512
LIST_HALF = HALF // 16
WG_SLOT = (None, "w_bf1", "slot_x", "slot_y", "slot_z", "slot_y", "slot_z", "slot_y")


def tile_list_crane_sway_page_kernel(tc, tab_words, tab_scales, offs, offs2, offs3, offs4, w1, w2,
                                              w3_words, w3_scales, gain, wgs, page0, rest, w4_words,
                                              w4_scales, wgo, page1, out):
    nc = tc.nc
    with ExitStack() as ctx:
        lists = ctx.enter_context(tc.tile_pool(name="lists", bufs=1))
        sb = ctx.enter_context(tc.tile_pool(name="sb", bufs=1))
        ps = ctx.enter_context(tc.psum_pool(name="ps", bufs=2))

        def tile(name, shape, dtype, tag=None, bufs=1):
            return sb.tile(shape, dtype, name=name, tag=tag or name, bufs=bufs, align_bytes=64)

        def half(h):
            return slice(h * HALF, (h + 1) * HALF)

        def list_half(lst, h):
            return lst[:, h * LIST_HALF:(h + 1) * LIST_HALF]

        def load_scale_rows(queue, plane, rows):
            for q in range(4):
                queue.dma_start(out=plane[32 * q:32 * q + 4].bitcast(I32), in_=rows[4 * q:4 * q + 4].bitcast(I32))

        idx1 = lists.tile([P, S // 16], U16, name="idx1")
        idx2 = lists.tile([P, S // 16], U16, name="idx2")
        idx3 = lists.tile([P, PK // 16], U16, name="idx3")
        idx4 = lists.tile([P, PK // 16], U16, name="idx4")

        tab_s = tile("tab_s", [P, T], U8)
        w3_s_raw = tile("w3_s_raw", [P, H], U8)
        w4_s = tile("w4_s", [P, 2, N], U8)
        one = tile("one", [P, 1], F32)
        one_b = tile("one_b", [P, 1], F32)
        nc.gpsimd.memset(tab_s[:, 0:T // 2].bitcast(I32), 0)
        nc.vector.memset(tab_s[:, T // 2:T].bitcast(I32), 0)
        nc.vector.memset(w3_s_raw[:].bitcast(I32), 0)
        nc.gpsimd.memset(one[:], 1.0)
        nc.gpsimd.memset(w4_s[:].rearrange("p a n -> p (a n)").bitcast(I32), 0)
        nc.scalar.activation(one_b[:], one[:], ACT.Sqrt)

        def load_w(w, which, b):
            raw = tile("w_raw%d_%d" % (which, b), [P, 4, HALF], F32, tag="w_raw%d" % which)
            nc.sync.dma_start(out=raw[:], in_=w[:, half(b)].rearrange("(p j) c -> p j c", j=4))
            return raw

        def cast_w(raw, which, b):
            grouped = tile("w_bf%d_%d" % (which, b), [P, 4 * HALF], BF16, tag="w_bf%d" % which)
            nc.scalar.copy(out=grouped[:].rearrange("p (t m j) -> p m t j", t=4, j=4),
                           in_=raw[:].rearrange("p j (m t) -> p m t j", t=4))
            return grouped

        gain_t = tile("gain_t", [P, 2, 4], F32)
        rest_t = tile("rest_t", [P, 2, 4], F32)
        w3_w_raw = tile("w3_w_raw", [P, 2 * H], U8)
        tab_w = tile("tab_w", [P, T], U32)
        wgs_rows = wgs.rearrange("(q t) j -> q t j", t=4)
        wgs_first = tile("wgs_first", [P, S], F32)
        page0_rows = page0.rearrange("(b p t) c -> b t p c", b=2, t=4)
        pages = [tile("page%d" % r, [P, T2], F32) for r in range(8)]
        nc.sync.dma_start(idx1[:], offs)
        nc.sync.dma_start(out=w3_w_raw[:].bitcast(I32), in_=w3_words[0].bitcast(I32))
        load_scale_rows(nc.sync, tab_s, tab_scales[0])
        w_raw = [load_w(w1, 0, 0), load_w(w2, 1, 0)]
        load_scale_rows(nc.sync, w3_s_raw, w3_scales[0])
        nc.sync.dma_start(out=tab_w[:].bitcast(I32), in_=tab_words[0].rearrange("p t i -> p (t i)").bitcast(I32))
        nc.sync.dma_start(out=gain_t[:], in_=gain.rearrange("(b p t) -> p b t", b=2, t=4))
        for q in range(4):
            nc.sync.dma_start(out=wgs_first[32 * q:32 * q + 32, :], in_=wgs_rows[:, 0, :])
        nc.sync.dma_start(out=pages[0][:], in_=page0_rows[0, 0])
        nc.sync.dma_start(idx2[:], offs2)

        v_s = [tile("v_s%d" % h, [P, HALF], U8) for h in range(2)]
        v_w = [tile("v_w%d" % h, [P, HALF], U32) for h in range(2)]
        w3_w = tile("w3_w", [P, 2 * H], U8)
        w3_s = tile("w3_s", [P, H], U8)
        nc.vector.tensor_copy(w3_w[:].rearrange("p (b t q e) -> p b q t e", b=2, t=4, e=2),
                              w3_w_raw[:].rearrange("p (b q t e) -> p b q t e", b=2, t=4, e=2))
        for h in range(2):
            nc.vector.tensor_copy(v_s[h][:], tab_s[:].indirect(list_half(idx1, h)))
        nc.vector.tensor_copy(w3_s[:].rearrange("p (b t q) -> p b t q", b=2, t=4),
                              w3_s_raw[:].rearrange("p (b q t) -> p b t q", b=2, t=4))

        w_s = tile("w_s", [P, 2, 2, HALF], U8)
        w_c = {}

        def quantize_w(grouped, b, tag):
            w_c[b] = tile("w_c%d" % b, [P, 2, HALF], U32, tag=tag)
            for which in range(2):
                nc.vector.quantize_mx(out=w_c[b][:, which, :].bitcast(FP8X4), scales=w_s[:, b, which, :],
                                      in_=grouped[which][:])

        quantize_w([cast_w(w_raw[0], 0, 0), cast_w(w_raw[1], 1, 0)], 0, "w_c0")
        for h in range(2):
            nc.vector.tensor_copy(v_w[h][:], tab_w[:].indirect(list_half(idx1, h)))

        wgs_other = tile("wgs_other", [P, 3, S], F32)
        for q in range(4):
            nc.sync.dma_start(out=wgs_other[32 * q:32 * q + 32], in_=wgs_rows[:, 1:4, :])
        nc.sync.dma_start(out=pages[1][:], in_=page0_rows[0, 1])
        nc.sync.dma_start(idx3[:], offs3)
        nc.sync.dma_start(out=rest_t[:], in_=rest.rearrange("(b p t) -> p b t", b=2, t=4))
        nc.sync.dma_start(idx4[:], offs4)
        w_raw = [load_w(w1, 0, 1), load_w(w2, 1, 1)]
        for r in range(2, 8):
            nc.sync.dma_start(out=pages[r][:], in_=page0_rows[r // 4, r % 4])
        load_scale_rows(nc.sync, w4_s, w4_scales.rearrange("a q n -> q a n"))
        w4_w = tile("w4_w", [P, 2, N], U32)
        nc.sync.dma_start(out=w4_w[:].bitcast(I32), in_=w4_words.rearrange("a p c i -> p a (c i)").bitcast(I32))
        wgo_t = tile("wgo_t", [P, PK], F32)
        nc.sync.dma_start(out=wgo_t[:], in_=wgo)
        outs = [tile("out%d" % n, [P, T2], F32) for n in range(4)]
        for n in range(4):
            nc.sync.dma_start(out=outs[n][:], in_=page1[n * P:(n + 1) * P, :])

        neg_rest = tile("neg_rest", [P, 8], F32)

        def largest(r):
            b, t = divmod(r, 4)
            cols = slice(t * P, (t + 1) * P)
            banks = []
            for h in range(2):
                pa = ps.tile([P, HALF], F32, name="pa%d_%d" % (r, h), tag="pa")
                pb = ps.tile([P, HALF], F32, name="pb%d_%d" % (r, h), tag="pb")
                pe = ps.tile([P, HALF], F32, name="pe%d_%d" % (r, h), tag="pe")
                for which, bank in ((0, pa), (1, pb)):
                    nc.tensor.matmul_mx(out=bank[:], lhsT=w_c[b][:, which, cols].bitcast(FP8X4),
                                        lhsT_scale=w_s[:, b, which, cols], rhs=v_w[h][:].bitcast(FP8X4),
                                        rhs_scale=v_s[h][:], start=True, stop=True)
                nc.tensor.matmul_mx(out=pe[:], lhsT=w3_w[:, 2 * r * P:2 * (r + 1) * P].bitcast(FP4X4),
                                    lhsT_scale=w3_s[:, r * P:(r + 1) * P], rhs=v_w[h][:].bitcast(FP8X4),
                                    rhs_scale=v_s[h][:], start=True, stop=True)
                if r == 0:
                    a_sb = a_first[:, half(h)]
                else:
                    a_sb = tile("a_sb%d_%d" % (r, h), [P, HALF], F32, tag="a_sb", bufs=2)[:]
                nc.scalar.copy(out=a_sb, in_=pa[:])
                banks.append((a_sb, pb, pe))
            return banks

        def maxima(tops, banks):
            for top, (a_sb, pb, pe) in zip(tops, banks):
                nc.vector.tensor_tensor(top, a_sb, pb[:], ALU.max)
            for top, (a_sb, pb, pe) in zip(tops, banks):
                nc.vector.tensor_tensor(top, top, pe[:], ALU.max)

        def weight(wg, r):
            b, t = divmod(r, 4)
            src = wgs_first[:] if t == 0 else wgs_other[:, t - 1, :]
            nc.scalar.activation(wg, src, ACT.Copy, scale=gain_t[:, b, t:t + 1])

        def against_rest(x_bf, picked, r):
            nc.scalar.activation(x_bf.rearrange("p (j t) -> p j t", t=4)[:, :, r % 4], picked, ACT.Identity,
                                 bias=neg_rest[:, r:r + 1])

        a_first = tile("a_first", [P, S], F32, tag="w_bf1")
        banks = largest(0)
        for h in range(2):
            top = tile("top0_%d" % h, [P, HALF], F32, tag=("top1", "slot_x")[h])
            wg = tile("wg0_%d" % h, [P, HALF], F32, tag=("slot_x", "w_bf0")[h])
            nc.gpsimd.tensor_scalar(wg[:], wgs_first[:, half(h)], gain_t[:, 0, 0:1], 0.0, ALU.mult, ALU.add)
            maxima([top[:]], banks[h:h + 1])
            nc.vector.tensor_tensor(pages[0][:].indirect(list_half(idx2, h)), top[:], wg[:], ALU.mult)
        x_bf = {}
        for r in range(8):
            if r > 0:
                wg = tile("wg%d" % r, [P, S], F32, tag=WG_SLOT[r])
                weight(wg[:], r)
                nc.vector.tensor_tensor(pages[r][:].indirect(idx2[:]), top[:], wg[:], ALU.mult)
            if r == 0:
                nc.gpsimd.tensor_scalar(neg_rest[:], rest_t[:].rearrange("p b t -> p (b t)"), -1.0, 0.0, ALU.mult, ALU.add)
                w_bf = [cast_w(w_raw[0], 0, 1)]
                x_bf[0] = tile("x_bf0", [P, 4 * PK], BF16, tag="w_raw0")
            if r == 1:
                w_bf.append(cast_w(w_raw[1], 1, 1))
            if r < 7:
                if r == 3:
                    x_bf[1, 0] = tile("x_bf1_0", [P, 4 * HALF], BF16, tag="w_bf0")
                banks = largest(r + 1)
                top = tile("top%d" % (r + 1), [P, S], F32, tag="top%d" % ((r + 1) % 2))
                maxima([top[:, half(0)], top[:, half(1)]], banks)
            if r == 2:
                quantize_w(w_bf, 1, "slot_x")
            if r < 2:
                picked = tile("picked%d" % r, [P, PK], F32, tag=("slot_y", "slot_z")[r])
            else:
                picked = tile("picked%d" % r, [P, PK], F32, tag="picked", bufs=2)
            if r < 4:
                nc.vector.tensor_copy(picked[:], pages[r][:].indirect(idx3[:]))
                against_rest(x_bf[0][:], picked[:], r)
            else:
                nc.vector.tensor_copy(picked[:, half(0)], pages[r][:].indirect(list_half(idx3, 0)))
                against_rest(x_bf[1, 0][:], picked[:, half(0)], r)

        x_c = [tile("x_c0", [P, PK], U32, tag="slot_y"), tile("x_c1", [P, PK], U32)]
        x_s = tile("x_s", [P, 2, PK], U8)

        def quantize_x(a, h, grouped):
            nc.vector.quantize_mx(out=x_c[a][:, half(h)].bitcast(FP8X4), scales=x_s[:, a, half(h)], in_=grouped)

        def late_gathers(rows, tag):
            late = tile("late%d" % rows[0], [P, 2, HALF], F32, tag=tag)
            for i, r in enumerate(rows):
                nc.vector.tensor_copy(late[:, i, :], pages[r][:].indirect(list_half(idx3, 1)))
            return late

        quantize_x(0, 0, x_bf[0][:, 0:4 * HALF])
        late45 = late_gathers((4, 5), "top1")
        quantize_x(1, 0, x_bf[1, 0][:])
        quantize_x(0, 1, x_bf[0][:, 4 * HALF:8 * HALF])
        late67 = late_gathers((6, 7), "w_bf0")

        def squares(n, h, tag, bufs):
            z = ps.tile([P, HALF], F32, name="z%d_%d" % (n, h), tag="z")
            cols = slice(n * P, (n + 1) * P)
            for a in range(2):
                nc.tensor.matmul_mx(out=z[:], lhsT=w4_w[:, a, cols].bitcast(FP8X4), lhsT_scale=w4_s[:, a, cols],
                                    rhs=x_c[a][:, half(h)].bitcast(FP8X4), rhs_scale=x_s[:, a, half(h)],
                                    start=(a == 0), stop=(a == 1))
            sq = tile("sq%d_%d" % (n, h), [P, HALF], F32, tag=tag, bufs=bufs)
            nc.scalar.activation(sq[:], z[:], ACT.Square)
            return sq

        def place(n, h, sq, tag):
            y = tile("y%d_%d" % (n, h), [P, HALF], F32, tag=tag)
            nc.scalar.activation(y[:], sq[:], ACT.Sqrt, bias=one_b[:])
            nc.vector.tensor_tensor(outs[n][:].indirect(list_half(idx4, h)), y[:], wgo_t[:, half(h)], ALU.mult)

        y_tags = ("y0", "y1", "y2", "y3")
        place(0, 0, squares(0, 0, "slot_z", 1), y_tags[0])
        for n in (1, 2):
            place(n, 0, squares(n, 0, "a_sb", 2), y_tags[n])
        sq_last = squares(3, 0, "a_sb", 2)
        x_bf[1, 1] = tile("x_bf1_1", [P, 4 * HALF], BF16, tag="slot_z")
        for r in range(4, 8):
            against_rest(x_bf[1, 1][:], (late45 if r < 6 else late67)[:, r % 2, :], r)
        quantize_x(1, 1, x_bf[1, 1][:])
        place(3, 0, sq_last, "slot_z")
        for n in range(4):
            place(n, 1, squares(n, 1, "a_sb", 2), y_tags[n])
            nc.sync.dma_start(out=out[n * P:(n + 1) * P, :], in_=outs[n][:])
